import numpy as np
import ml_dtypes


def mxq(x, axis, fmt="e4m3"):
    dtype, down = {"e4m3": (ml_dtypes.float8_e4m3fn, 7), "e5m2": (ml_dtypes.float8_e5m2, 14)}[fmt]
    v = np.moveaxis(np.asarray(x, np.float32).astype(ml_dtypes.bfloat16).astype(np.float64), axis, -1)
    blocks = v.reshape(v.shape[:-1] + (-1, 32))
    amax = np.abs(blocks).max(-1, keepdims=True)
    byte = np.maximum(np.where(amax > 0, np.frexp(amax)[1] - 1 + 127, 0) - down, 1)
    scale = np.exp2(byte - 127.0)
    codes = (blocks / scale).astype(np.float32).astype(dtype).astype(np.float64)
    return np.moveaxis((codes * scale).reshape(v.shape), -1, axis)


WIDE = False


def mx_kscale(k):
    if not WIDE:
        return np.ones(k)
    levels = np.array([10, -10, 5, -5, 0])
    if k % 512:
        return np.exp2(np.random.permutation(np.resize(levels, k // 32))).repeat(32)
    a = np.empty((k // 512, 16))
    for p in range(k // 512):
        a[p, :8] = np.random.permutation(np.resize(levels, 8))
        for g in range(8):
            far = levels[np.abs(levels - a[p, g]) >= 10]
            a[p, g + 8] = far[np.random.randint(len(far))]
    return np.exp2(a.ravel()).repeat(32)


def f64(x):
    return np.asarray(x).astype(np.float64)


def striped(idx):
    return np.tile(idx.reshape(-1, 16).T, (8, 1)).astype(np.uint16)


def unstriped(offs):
    return offs[:16].T.reshape(-1).astype(np.int64)


def pack_weight(w):
    k, n = w.shape
    w = f64(np.asarray(w, np.float32).astype(ml_dtypes.bfloat16)).reshape(k // 32, 32, n)
    amax = np.abs(w).max(1)
    byte = np.clip(np.where(amax > 0, np.frexp(amax)[1] - 1 + 127 - 7, 1), 1, 254)
    scaled = (w * np.exp2(127.0 - byte)[:, None, :]).reshape(k, n).astype(np.float32)
    words = np.ascontiguousarray(scaled.reshape(k // 512, 128, 4, n).transpose(0, 1, 3, 2)).astype(ml_dtypes.float8_e4m3fn).view(np.uint8)
    return words, np.ascontiguousarray(byte.astype(np.uint8).reshape(k // 512, 16, n))


def unpack_weight(words, scales):
    g, p, n, _ = words.shape
    vals = np.ascontiguousarray(words).view(ml_dtypes.float8_e4m3fn).astype(np.float64) * np.repeat(np.exp2(scales.astype(np.float64) - 127.0), 8, axis=1)[..., None]
    return vals.transpose(0, 1, 3, 2).reshape(g * 512, n)


K, T, S, V, N = 1024, 1024, 512, 256, 256


def setup_inputs():
    n = np.random.standard_normal
    s = mx_kscale(K)[:, None]
    packed_xT = pack_weight(n((K, T)) * s)
    return {
        "x_words": packed_xT[0],
        "x_scales": packed_xT[1],
        "w1": (n((K, N)) / np.sqrt(K) / s).astype(np.float32),
        "offs": striped(np.random.permutation(T)[:S]),
        "win": striped(np.random.permutation(S)[:V]),
        "lose": striped(np.random.permutation(S)[:V]),
    }


def reference(x_words, x_scales, w1, offs, win, lose):
    xq = unpack_weight(x_words, x_scales)[:, unstriped(offs)]
    y = mxq(f64(w1), 0, "e4m3").T @ xq
    return np.tanh(y[:, unstriped(win)] - y[:, unstriped(lose)])

@@ -1,0 +1,136 @@
+from contextlib import ExitStack
+
+import concourse.mybir as mybir
+
+K, T, S, V, N = 1024, 1024, 512, 256, 256
+FLOPS = 2 * K * S * N
+
+F32 = mybir.dt.float32
+BF16 = mybir.dt.bfloat16
+I32 = mybir.dt.int32
+U32 = mybir.dt.uint32
+U16 = mybir.dt.uint16
+U8 = mybir.dt.uint8
+FP8X4 = mybir.dt.float8_e4m3fn_x4
+TANH = mybir.ActivationFunctionType.Tanh
+SUBTRACT = mybir.AluOpType.subtract
+
+P = 128
+PACK = 4
+K_PASS = P * PACK
+HALF = S // 2
+VH = V // 2
+
+
+def tile_picked_ranknet_tanh_p_kernel(tc, x_words, x_scales, w1, offs, win, lose, out):
+    nc = tc.nc
+    with ExitStack() as ctx:
+        keep = ctx.enter_context(tc.tile_pool(name="keep", bufs=1))
+        psum = ctx.enter_context(tc.psum_pool(name="psum", bufs=1))
+
+        offs_t = keep.tile([P, S // 16], U16, name="offs_t")
+        win_t = keep.tile([P, V // 16], U16, name="win_t")
+        lose_t = keep.tile([P, V // 16], U16, name="lose_t")
+        words = [keep.tile([P, T], I32, name=f"words{z}", align_bytes=64) for z in range(2)]
+        planes = keep.tile([P, T], U8, name="planes", align_bytes=64)
+        raw = {(m, z): keep.tile([P, PACK, P], F32, name=f"raw{m}{z}", align_bytes=64) for m in range(2) for z in range(2)}
+        grouped = {(m, z): keep.tile([P, P * PACK], BF16, name=f"grouped{m}{z}", align_bytes=64) for m in range(2) for z in range(2)}
+        w_codes = {(m, z): keep.tile([P, P], U32, name=f"w_codes{m}{z}", align_bytes=64) for m in range(2) for z in range(2)}
+        w_scales = {(m, z): keep.tile([P, P], U8, name=f"w_scales{m}{z}", align_bytes=64) for m in range(2) for z in range(2)}
+        picked = {(z, h): keep.tile([P, HALF], U32, name=f"picked{z}{h}", align_bytes=64) for z in range(2) for h in range(2)}
+        picked_planes = keep.tile([P, S], U8, name="picked_planes", align_bytes=64)
+        banks = {(m, h): psum.tile([P, HALF], F32, name=f"bank{m}{h}") for m in range(2) for h in range(2)}
+        y = [keep.tile([P, S], F32, name=f"y{m}", align_bytes=64) for m in range(2)]
+        zero = keep.tile([P, 1], F32, name="zero")
+        bias = keep.tile([P, 1], F32, name="bias")
+
+        def load_words(z):
+            nc.sync.dma_start(out=words[z][:], in_=x_words[z].rearrange("p n t -> p (n t)").bitcast(I32))
+
+        def load_w(m, z):
+            rows = w1[z * K_PASS : (z + 1) * K_PASS, m * P : (m + 1) * P]
+            nc.sync.dma_start(out=raw[m, z][:], in_=rows.rearrange("(p j) c -> p j c", j=PACK))
+
+        def interleave(engine_copy, m, z):
+            engine_copy(
+                grouped[m, z][:].rearrange("p (c i t) -> p c t i", i=4, t=PACK),
+                raw[m, z][:].rearrange("p t (c i) -> p c t i", i=4),
+            )
+
+        def quantize(m, z):
+            nc.vector.quantize_mx(out=w_codes[m, z][:].bitcast(FP8X4), scales=w_scales[m, z][:], in_=grouped[m, z][:])
+
+        def gather_words(z, h):
+            cols = slice(h * HALF // 16, (h + 1) * HALF // 16)
+            nc.vector.tensor_copy(picked[z, h][:], words[z][:].bitcast(U32).indirect(offs_t[:, cols]))
+
+        def multiply(m, z, h):
+            nc.tensor.matmul_mx(
+                out=banks[m, h][:],
+                lhsT=w_codes[m, z][:].bitcast(FP8X4),
+                lhsT_scale=w_scales[m, z][:],
+                rhs=picked[z, h][:].bitcast(FP8X4),
+                rhs_scale=picked_planes[4 * z : P, h * HALF : (h + 1) * HALF],
+                start=(z == 0),
+                stop=(z == 1),
+            )
+
+        def to_sbuf(m, h):
+            nc.scalar.copy(y[m][:, h * HALF : (h + 1) * HALF], banks[m, h][:])
+
+        def compare(m):
+            losers = [keep.tile([P, VH], F32, name=f"losers{m}{u}", align_bytes=64) for u in range(2)]
+            margin = [keep.tile([P, VH], F32, name=f"margin{m}{u}", align_bytes=64) for u in range(2)]
+            result = [keep.tile([P, VH], F32, name=f"result{m}{u}", align_bytes=64) for u in range(2)]
+            cols = [slice(u * VH // 16, (u + 1) * VH // 16) for u in range(2)]
+            for u in range(2):
+                nc.vector.tensor_copy(losers[u][:], y[m][:].indirect(lose_t[:, cols[u]]))
+            for u in range(2):
+                nc.vector.tensor_tensor(margin[u][:], y[m][:].indirect(win_t[:, cols[u]]), losers[u][:], SUBTRACT)
+                nc.scalar.activation(result[u][:], margin[u][:], TANH, bias=bias[:])
+                nc.sync.dma_start(out=out[m * P : (m + 1) * P, u * VH : (u + 1) * VH], in_=result[u][:])
+
+        nc.vector.memset(planes[:].bitcast(I32), 0)
+        nc.vector.memset(zero[:], 0.0)
+        nc.scalar.activation(bias[:], zero[:], TANH)
+
+        load_words(0)
+        nc.sync.dma_start(offs_t[:], offs)
+        for q in range(4):
+            nc.sync.dma_start(
+                out=planes[32 * q : 32 * q + 8, :].bitcast(I32),
+                in_=x_scales[:, 4 * q : 4 * q + 4, :].bitcast(I32),
+            )
+        load_w(0, 0)
+        load_w(0, 1)
+        load_words(1)
+        load_w(1, 0)
+        load_w(1, 1)
+        nc.sync.dma_start(lose_t[:], lose)
+        nc.sync.dma_start(win_t[:], win)
+
+        gather_words(0, 0)
+        gather_words(0, 1)
+        nc.vector.tensor_copy(picked_planes[:], planes[:].indirect(offs_t[:]))
+        interleave(nc.scalar.copy, 0, 0)
+        interleave(nc.scalar.copy, 0, 1)
+        quantize(0, 0)
+        quantize(0, 1)
+        multiply(0, 0, 0)
+        multiply(0, 0, 1)
+        for h in range(2):
+            gather_words(1, h)
+            multiply(0, 1, h)
+        interleave(nc.scalar.copy, 1, 0)
+        for h in range(2):
+            to_sbuf(0, h)
+        quantize(1, 0)
+        interleave(nc.vector.tensor_copy, 1, 1)
+        multiply(1, 0, 0)
+        multiply(1, 0, 1)
+        quantize(1, 1)
+        for h in range(2):
+            multiply(1, 1, h)
+            to_sbuf(1, h)
+        compare(0)
+        compare(1)

@@ -18,8 +18,6 @@ SUBTRACT = mybir.AluOpType.subtract
 P = 128
 PACK = 4
 K_PASS = P * PACK
-HALF = S // 2
-VH = V // 2
 
 
 def tile_picked_ranknet_tanh_p_kernel(tc, x_words, x_scales, w1, offs, win, lose, out):
@@ -34,103 +32,131 @@ def tile_picked_ranknet_tanh_p_kernel(tc, x_words, x_scales, w1, offs, win, lose
         words = [keep.tile([P, T], I32, name=f"words{z}", align_bytes=64) for z in range(2)]
         planes = keep.tile([P, T], U8, name="planes", align_bytes=64)
         raw = {(m, z): keep.tile([P, PACK, P], F32, name=f"raw{m}{z}", align_bytes=64) for m in range(2) for z in range(2)}
-        grouped = {(m, z): keep.tile([P, P * PACK], BF16, name=f"grouped{m}{z}", align_bytes=64) for m in range(2) for z in range(2)}
-        w_codes = {(m, z): keep.tile([P, P], U32, name=f"w_codes{m}{z}", align_bytes=64) for m in range(2) for z in range(2)}
-        w_scales = {(m, z): keep.tile([P, P], U8, name=f"w_scales{m}{z}", align_bytes=64) for m in range(2) for z in range(2)}
-        picked = {(z, h): keep.tile([P, HALF], U32, name=f"picked{z}{h}", align_bytes=64) for z in range(2) for h in range(2)}
+        wide = [keep.tile([P, PACK, N], F32, name=f"wide{z}", align_bytes=64) for z in range(2)]
+        grouped = keep.tile([P, 4 * P * PACK], BF16, name="grouped", align_bytes=64)
+        w_codes = keep.tile([P, 4 * P], U32, name="w_codes", align_bytes=64)
+        w_scales = keep.tile([P, 4 * P], U8, name="w_scales", align_bytes=64)
+        picked = [keep.tile([P, S], U32, name=f"picked{z}", align_bytes=64) for z in range(2)]
         picked_planes = keep.tile([P, S], U8, name="picked_planes", align_bytes=64)
-        banks = {(m, h): psum.tile([P, HALF], F32, name=f"bank{m}{h}") for m in range(2) for h in range(2)}
+        pieces = {0: [[0,256],[256,384],[384,512]], 1: [[0,256],[256,384],[384,512]]}
+        banks = {(m, a): psum.tile([P, b - a], F32, name=f"bank{m}_{a}") for m in range(2) for a, b in pieces[m]}
         y = [keep.tile([P, S], F32, name=f"y{m}", align_bytes=64) for m in range(2)]
+        losers = [keep.tile([P, V], F32, name=f"losers{m}", align_bytes=64) for m in range(2)]
+        margin = [keep.tile([P, V], F32, name=f"margin{m}", align_bytes=64) for m in range(2)]
+        result = [keep.tile([P, V], F32, name=f"result{m}", align_bytes=64) for m in range(2)]
         zero = keep.tile([P, 1], F32, name="zero")
         bias = keep.tile([P, 1], F32, name="bias")
+        slot = {(0, 0): 0, (0, 1): 1, (1, 0): 2, (1, 1): 3}
+        source = {}
 
         def load_words(z):
             nc.sync.dma_start(out=words[z][:], in_=x_words[z].rearrange("p n t -> p (n t)").bitcast(I32))
 
+        def load_scales(queue=nc.sync):
+            for q in range(4):
+                queue.dma_start(
+                    out=planes[32 * q : 32 * q + 8, :].bitcast(I32),
+                    in_=x_scales[:, 4 * q : 4 * q + 4, :].bitcast(I32),
+                )
+
         def load_w(m, z):
             rows = w1[z * K_PASS : (z + 1) * K_PASS, m * P : (m + 1) * P]
             nc.sync.dma_start(out=raw[m, z][:], in_=rows.rearrange("(p j) c -> p j c", j=PACK))
+            source[m, z] = raw[m, z][:]
 
-        def interleave(engine_copy, m, z):
+        def load_wide(z):
+            rows = w1[z * K_PASS : (z + 1) * K_PASS, :]
+            nc.sync.dma_start(out=wide[z][:], in_=rows.rearrange("(p j) c -> p j c", j=PACK))
+            for m in range(2):
+                source[m, z] = wide[z][:, :, m * P : (m + 1) * P]
+
+        def interleave(engine_copy, m, z, a=0, b=P):
+            s = slot[m, z]
             engine_copy(
-                grouped[m, z][:].rearrange("p (c i t) -> p c t i", i=4, t=PACK),
-                raw[m, z][:].rearrange("p t (c i) -> p c t i", i=4),
+                grouped[:, (s * P + a) * PACK : (s * P + b) * PACK].rearrange("p (c i t) -> p c t i", i=4, t=PACK),
+                source[m, z][:, :, a:b].rearrange("p t (c i) -> p c t i", i=4),
             )
 
-        def quantize(m, z):
-            nc.vector.quantize_mx(out=w_codes[m, z][:].bitcast(FP8X4), scales=w_scales[m, z][:], in_=grouped[m, z][:])
+        def quantize(s, count=1):
+            cols = slice(s * P, (s + count) * P)
+            nc.vector.quantize_mx(
+                out=w_codes[:, cols].bitcast(FP8X4), scales=w_scales[:, cols], in_=grouped[:, s * P * PACK : (s + count) * P * PACK]
+            )
 
-        def gather_words(z, h):
-            cols = slice(h * HALF // 16, (h + 1) * HALF // 16)
-            nc.vector.tensor_copy(picked[z, h][:], words[z][:].bitcast(U32).indirect(offs_t[:, cols]))
+        def gather_words(z, a, b):
+            nc.vector.tensor_copy(picked[z][:, a:b], words[z][:].bitcast(U32).indirect(offs_t[:, a // 16 : b // 16]))
 
-        def multiply(m, z, h):
+        def gather_planes(a, b):
+            nc.vector.tensor_copy(picked_planes[:, a:b], planes[:].indirect(offs_t[:, a // 16 : b // 16]))
+
+        def multiply(m, z, a, b, first=0):
+            cols = slice(slot[m, z] * P, (slot[m, z] + 1) * P)
             nc.tensor.matmul_mx(
-                out=banks[m, h][:],
-                lhsT=w_codes[m, z][:].bitcast(FP8X4),
-                lhsT_scale=w_scales[m, z][:],
-                rhs=picked[z, h][:].bitcast(FP8X4),
-                rhs_scale=picked_planes[4 * z : P, h * HALF : (h + 1) * HALF],
-                start=(z == 0),
-                stop=(z == 1),
+                out=banks[m, a][:],
+                lhsT=w_codes[:, cols].bitcast(FP8X4),
+                lhsT_scale=w_scales[:, cols],
+                rhs=picked[z][:, a:b].bitcast(FP8X4),
+                rhs_scale=picked_planes[4 * z : P, a:b],
+                start=(z == first),
+                stop=(z != first),
             )
 
-        def to_sbuf(m, h):
-            nc.scalar.copy(y[m][:, h * HALF : (h + 1) * HALF], banks[m, h][:])
+        def to_sbuf(m, a, b, engine_copy=nc.scalar.copy):
+            engine_copy(y[m][:, a:b], banks[m, a][:])
 
-        def compare(m):
-            losers = [keep.tile([P, VH], F32, name=f"losers{m}{u}", align_bytes=64) for u in range(2)]
-            margin = [keep.tile([P, VH], F32, name=f"margin{m}{u}", align_bytes=64) for u in range(2)]
-            result = [keep.tile([P, VH], F32, name=f"result{m}{u}", align_bytes=64) for u in range(2)]
-            cols = [slice(u * VH // 16, (u + 1) * VH // 16) for u in range(2)]
-            for u in range(2):
-                nc.vector.tensor_copy(losers[u][:], y[m][:].indirect(lose_t[:, cols[u]]))
-            for u in range(2):
-                nc.vector.tensor_tensor(margin[u][:], y[m][:].indirect(win_t[:, cols[u]]), losers[u][:], SUBTRACT)
-                nc.scalar.activation(result[u][:], margin[u][:], TANH, bias=bias[:])
-                nc.sync.dma_start(out=out[m * P : (m + 1) * P, u * VH : (u + 1) * VH], in_=result[u][:])
+        def fetch_losers(m, a, b):
+            nc.vector.tensor_copy(losers[m][:, a:b], y[m][:].indirect(lose_t[:, a // 16 : b // 16]))
+
+        def subtract(m, a, b):
+            nc.vector.tensor_tensor(margin[m][:, a:b], y[m][:].indirect(win_t[:, a // 16 : b // 16]), losers[m][:, a:b], SUBTRACT)
+
+        def finish(m, a, b, queue=nc.sync):
+            nc.scalar.activation(result[m][:, a:b], margin[m][:, a:b], TANH, bias=bias[:])
+            queue.dma_start(out=out[m * P : (m + 1) * P, a:b], in_=result[m][:, a:b])
+
 
         nc.vector.memset(planes[:].bitcast(I32), 0)
         nc.vector.memset(zero[:], 0.0)
         nc.scalar.activation(bias[:], zero[:], TANH)
-
-        load_words(0)
         nc.sync.dma_start(offs_t[:], offs)
-        for q in range(4):
-            nc.sync.dma_start(
-                out=planes[32 * q : 32 * q + 8, :].bitcast(I32),
-                in_=x_scales[:, 4 * q : 4 * q + 4, :].bitcast(I32),
-            )
+        load_words(0)
+        nc.sync.dma_start(lose_t[:], lose)
+        load_scales()
         load_w(0, 0)
         load_w(0, 1)
         load_words(1)
         load_w(1, 0)
         load_w(1, 1)
-        nc.sync.dma_start(lose_t[:], lose)
         nc.sync.dma_start(win_t[:], win)
 
-        gather_words(0, 0)
-        gather_words(0, 1)
-        nc.vector.tensor_copy(picked_planes[:], planes[:].indirect(offs_t[:]))
+        gather_words(0, 0, 512)
+        gather_planes(0, 512)
         interleave(nc.scalar.copy, 0, 0)
         interleave(nc.scalar.copy, 0, 1)
-        quantize(0, 0)
-        quantize(0, 1)
-        multiply(0, 0, 0)
-        multiply(0, 0, 1)
-        for h in range(2):
-            gather_words(1, h)
-            multiply(0, 1, h)
+        quantize(0, 2)
+        for a, b in pieces[0]:
+            multiply(0, 0, a, b)
         interleave(nc.scalar.copy, 1, 0)
-        for h in range(2):
-            to_sbuf(0, h)
-        quantize(1, 0)
+        for a, b in pieces[0]:
+            gather_words(1, a, b)
+            multiply(0, 1, a, b)
+            to_sbuf(0, a, b)
+        quantize(2)
         interleave(nc.vector.tensor_copy, 1, 1)
-        multiply(1, 0, 0)
-        multiply(1, 0, 1)
-        quantize(1, 1)
-        for h in range(2):
-            multiply(1, 1, h)
-            to_sbuf(1, h)
-        compare(0)
-        compare(1)
+        for a, b in pieces[1]:
+            multiply(1, 0, a, b)
+        quantize(3)
+        for a, b in pieces[1]:
+            multiply(1, 1, a, b)
+            to_sbuf(1, a, b)
+        fetch_losers(0, 0, 128)
+        fetch_losers(0, 128, 256)
+        subtract(0, 0, 128)
+        subtract(0, 128, 256)
+        finish(0, 0, 256)
+        fetch_losers(1, 0, 192)
+        fetch_losers(1, 192, 256)
+        subtract(1, 0, 192)
+        finish(1, 0, 192)
+        subtract(1, 192, 256)
+        finish(1, 192, 256)

@@ -31,17 +31,17 @@ def tile_picked_ranknet_tanh_p_kernel(tc, x_words, x_scales, w1, offs, win, lose
         lose_t = keep.tile([P, V // 16], U16, name="lose_t")
         words = [keep.tile([P, T], I32, name=f"words{z}", align_bytes=64) for z in range(2)]
         planes = keep.tile([P, T], U8, name="planes", align_bytes=64)
-        raw = {(m, z): keep.tile([P, PACK, P], F32, name=f"raw{m}{z}", align_bytes=64) for m in range(2) for z in range(2)}
+        raw = {(m, z): keep.tile([P, PACK, P], F32, name=f"raw{m}{z}", tag=f"raw{m}{z}", align_bytes=64) for m in range(2) for z in range(2)}
         wide = [keep.tile([P, PACK, N], F32, name=f"wide{z}", align_bytes=64) for z in range(2)]
         grouped = keep.tile([P, 4 * P * PACK], BF16, name="grouped", align_bytes=64)
         w_codes = keep.tile([P, 4 * P], U32, name="w_codes", align_bytes=64)
         w_scales = keep.tile([P, 4 * P], U8, name="w_scales", align_bytes=64)
         picked = [keep.tile([P, S], U32, name=f"picked{z}", align_bytes=64) for z in range(2)]
         picked_planes = keep.tile([P, S], U8, name="picked_planes", align_bytes=64)
-        pieces = {0: [[0,256],[256,384],[384,512]], 1: [[0,256],[256,384],[384,512]]}
+        pieces = {0: [[0,256],[256,384],[384,512]], 1: [[0,128],[128,256],[256,384],[384,512]]}
         banks = {(m, a): psum.tile([P, b - a], F32, name=f"bank{m}_{a}") for m in range(2) for a, b in pieces[m]}
         y = [keep.tile([P, S], F32, name=f"y{m}", align_bytes=64) for m in range(2)]
-        losers = [keep.tile([P, V], F32, name=f"losers{m}", align_bytes=64) for m in range(2)]
+        losers = {1: keep.tile([P, V], F32, name="losers1", align_bytes=64)}
         margin = [keep.tile([P, V], F32, name=f"margin{m}", align_bytes=64) for m in range(2)]
         result = [keep.tile([P, V], F32, name=f"result{m}", align_bytes=64) for m in range(2)]
         zero = keep.tile([P, 1], F32, name="zero")
@@ -118,17 +118,16 @@ def tile_picked_ranknet_tanh_p_kernel(tc, x_words, x_scales, w1, offs, win, lose
         nc.vector.memset(planes[:].bitcast(I32), 0)
         nc.vector.memset(zero[:], 0.0)
         nc.scalar.activation(bias[:], zero[:], TANH)
-        nc.sync.dma_start(offs_t[:], offs)
         load_words(0)
-        nc.sync.dma_start(lose_t[:], lose)
-        load_scales()
+        nc.sync.dma_start(offs_t[:], offs)
         load_w(0, 0)
+        load_scales()
         load_w(0, 1)
         load_words(1)
         load_w(1, 0)
         load_w(1, 1)
+        nc.sync.dma_start(lose_t[:], lose)
         nc.sync.dma_start(win_t[:], win)
-
         gather_words(0, 0, 512)
         gather_planes(0, 512)
         interleave(nc.scalar.copy, 0, 0)
@@ -141,14 +140,21 @@ def tile_picked_ranknet_tanh_p_kernel(tc, x_words, x_scales, w1, offs, win, lose
             gather_words(1, a, b)
             multiply(0, 1, a, b)
             to_sbuf(0, a, b)
+        interleave(nc.vector.tensor_copy, 1, 1, 0, 64)
         quantize(2)
-        interleave(nc.vector.tensor_copy, 1, 1)
+        late = keep.tile([P, 64 * PACK], BF16, name="late", tag="raw10", align_bytes=64)
+        nc.vector.tensor_copy(
+            late[:].rearrange("p (c i t) -> p c t i", i=4, t=PACK),
+            raw[1, 1][:, :, 64:128].rearrange("p t (c i) -> p c t i", i=4),
+        )
         for a, b in pieces[1]:
             multiply(1, 0, a, b)
-        quantize(3)
+        nc.vector.quantize_mx(out=w_codes[:, 384:448].bitcast(FP8X4), scales=w_scales[:, 384:448], in_=grouped[:, 384 * PACK : 448 * PACK])
+        nc.vector.quantize_mx(out=w_codes[:, 448:512].bitcast(FP8X4), scales=w_scales[:, 448:512], in_=late[:])
         for a, b in pieces[1]:
             multiply(1, 1, a, b)
             to_sbuf(1, a, b)
+        losers[0] = keep.tile([P, V], F32, name="losers0", tag="raw11", align_bytes=64)
         fetch_losers(0, 0, 128)
         fetch_losers(0, 128, 256)
         subtract(0, 0, 128)

@@ -18,6 +18,11 @@ SUBTRACT = mybir.AluOpType.subtract
 P = 128
 PACK = 4
 K_PASS = P * PACK
+PER_COLUMN = 16
+WALK = 4
+HALF = P // 2
+
+RANGES = {0: [(0, 256), (256, 384), (384, 512)], 1: [(a, a + P) for a in range(0, S, P)]}
 
 
 def tile_picked_ranknet_tanh_p_kernel(tc, x_words, x_scales, w1, offs, win, lose, out):
@@ -26,143 +31,150 @@ def tile_picked_ranknet_tanh_p_kernel(tc, x_words, x_scales, w1, offs, win, lose
         keep = ctx.enter_context(tc.tile_pool(name="keep", bufs=1))
         psum = ctx.enter_context(tc.psum_pool(name="psum", bufs=1))
 
-        offs_t = keep.tile([P, S // 16], U16, name="offs_t")
-        win_t = keep.tile([P, V // 16], U16, name="win_t")
-        lose_t = keep.tile([P, V // 16], U16, name="lose_t")
+        offs_t = keep.tile([P, S // PER_COLUMN], U16, name="offs_t")
+        win_t = keep.tile([P, V // PER_COLUMN], U16, name="win_t")
+        lose_t = keep.tile([P, V // PER_COLUMN], U16, name="lose_t")
         words = [keep.tile([P, T], I32, name=f"words{z}", align_bytes=64) for z in range(2)]
-        planes = keep.tile([P, T], U8, name="planes", align_bytes=64)
-        raw = {(m, z): keep.tile([P, PACK, P], F32, name=f"raw{m}{z}", tag=f"raw{m}{z}", align_bytes=64) for m in range(2) for z in range(2)}
-        wide = [keep.tile([P, PACK, N], F32, name=f"wide{z}", align_bytes=64) for z in range(2)]
+        scale_rows = keep.tile([P, T], U8, name="scale_rows", align_bytes=64)
+        raw = {
+            (m, z): keep.tile([P, PACK, P], F32, name=f"raw{m}{z}", tag=f"raw{m}{z}", align_bytes=64)
+            for m in range(2)
+            for z in range(2)
+        }
         grouped = keep.tile([P, 4 * P * PACK], BF16, name="grouped", align_bytes=64)
         w_codes = keep.tile([P, 4 * P], U32, name="w_codes", align_bytes=64)
         w_scales = keep.tile([P, 4 * P], U8, name="w_scales", align_bytes=64)
         picked = [keep.tile([P, S], U32, name=f"picked{z}", align_bytes=64) for z in range(2)]
-        picked_planes = keep.tile([P, S], U8, name="picked_planes", align_bytes=64)
-        pieces = {0: [[0,256],[256,384],[384,512]], 1: [[0,128],[128,256],[256,384],[384,512]]}
-        banks = {(m, a): psum.tile([P, b - a], F32, name=f"bank{m}_{a}") for m in range(2) for a, b in pieces[m]}
+        picked_scales = keep.tile([P, S], U8, name="picked_scales", align_bytes=64)
+        banks = {(m, a): psum.tile([P, b - a], F32, name=f"bank{m}_{a}") for m in range(2) for a, b in RANGES[m]}
         y = [keep.tile([P, S], F32, name=f"y{m}", align_bytes=64) for m in range(2)]
         losers = {1: keep.tile([P, V], F32, name="losers1", align_bytes=64)}
         margin = [keep.tile([P, V], F32, name=f"margin{m}", align_bytes=64) for m in range(2)]
         result = [keep.tile([P, V], F32, name=f"result{m}", align_bytes=64) for m in range(2)]
         zero = keep.tile([P, 1], F32, name="zero")
         bias = keep.tile([P, 1], F32, name="bias")
-        slot = {(0, 0): 0, (0, 1): 1, (1, 0): 2, (1, 1): 3}
-        source = {}
+
+        def entries(list_tile, a, b):
+            return list_tile[:, a // PER_COLUMN : b // PER_COLUMN]
+
+        def first_column(m, z):
+            return (2 * m + z) * P
 
         def load_words(z):
             nc.sync.dma_start(out=words[z][:], in_=x_words[z].rearrange("p n t -> p (n t)").bitcast(I32))
 
-        def load_scales(queue=nc.sync):
+        def load_scale_rows():
             for q in range(4):
-                queue.dma_start(
-                    out=planes[32 * q : 32 * q + 8, :].bitcast(I32),
+                nc.sync.dma_start(
+                    out=scale_rows[32 * q : 32 * q + 8, :].bitcast(I32),
                     in_=x_scales[:, 4 * q : 4 * q + 4, :].bitcast(I32),
                 )
 
-        def load_w(m, z):
+        def load_piece(m, z):
             rows = w1[z * K_PASS : (z + 1) * K_PASS, m * P : (m + 1) * P]
-            nc.sync.dma_start(out=raw[m, z][:], in_=rows.rearrange("(p j) c -> p j c", j=PACK))
-            source[m, z] = raw[m, z][:]
+            nc.sync.dma_start(out=raw[m, z][:], in_=rows.rearrange("(p t) c -> p t c", t=PACK))
 
-        def load_wide(z):
-            rows = w1[z * K_PASS : (z + 1) * K_PASS, :]
-            nc.sync.dma_start(out=wide[z][:], in_=rows.rearrange("(p j) c -> p j c", j=PACK))
-            for m in range(2):
-                source[m, z] = wide[z][:, :, m * P : (m + 1) * P]
+        def grouped_columns(a, b):
+            return grouped[:, a * PACK : b * PACK]
 
-        def interleave(engine_copy, m, z, a=0, b=P):
-            s = slot[m, z]
+        def interleave(engine_copy, target, source):
             engine_copy(
-                grouped[:, (s * P + a) * PACK : (s * P + b) * PACK].rearrange("p (c i t) -> p c t i", i=4, t=PACK),
-                source[m, z][:, :, a:b].rearrange("p t (c i) -> p c t i", i=4),
+                target.rearrange("p (c i t) -> p c t i", i=WALK, t=PACK),
+                source.rearrange("p t (c i) -> p c t i", i=WALK),
             )
 
-        def quantize(s, count=1):
-            cols = slice(s * P, (s + count) * P)
-            nc.vector.quantize_mx(
-                out=w_codes[:, cols].bitcast(FP8X4), scales=w_scales[:, cols], in_=grouped[:, s * P * PACK : (s + count) * P * PACK]
-            )
+        def interleave_on_scalar(m, z):
+            a = first_column(m, z)
+            interleave(nc.scalar.copy, grouped_columns(a, a + P), raw[m, z][:])
+
+        def quantize(a, b, source):
+            nc.vector.quantize_mx(out=w_codes[:, a:b].bitcast(FP8X4), scales=w_scales[:, a:b], in_=source)
 
         def gather_words(z, a, b):
-            nc.vector.tensor_copy(picked[z][:, a:b], words[z][:].bitcast(U32).indirect(offs_t[:, a // 16 : b // 16]))
+            nc.vector.tensor_copy(picked[z][:, a:b], words[z][:].bitcast(U32).indirect(entries(offs_t, a, b)))
 
-        def gather_planes(a, b):
-            nc.vector.tensor_copy(picked_planes[:, a:b], planes[:].indirect(offs_t[:, a // 16 : b // 16]))
-
-        def multiply(m, z, a, b, first=0):
-            cols = slice(slot[m, z] * P, (slot[m, z] + 1) * P)
+        def multiply(m, z, a, b):
+            cols = slice(first_column(m, z), first_column(m, z) + P)
             nc.tensor.matmul_mx(
                 out=banks[m, a][:],
                 lhsT=w_codes[:, cols].bitcast(FP8X4),
                 lhsT_scale=w_scales[:, cols],
                 rhs=picked[z][:, a:b].bitcast(FP8X4),
-                rhs_scale=picked_planes[4 * z : P, a:b],
-                start=(z == first),
-                stop=(z != first),
+                rhs_scale=picked_scales[4 * z : P, a:b],
+                start=(z == 0),
+                stop=(z == 1),
             )
 
-        def to_sbuf(m, a, b, engine_copy=nc.scalar.copy):
-            engine_copy(y[m][:, a:b], banks[m, a][:])
+        def to_sbuf(m, a, b):
+            nc.scalar.copy(y[m][:, a:b], banks[m, a][:])
 
         def fetch_losers(m, a, b):
-            nc.vector.tensor_copy(losers[m][:, a:b], y[m][:].indirect(lose_t[:, a // 16 : b // 16]))
+            nc.vector.tensor_copy(losers[m][:, a:b], y[m][:].indirect(entries(lose_t, a, b)))
 
         def subtract(m, a, b):
-            nc.vector.tensor_tensor(margin[m][:, a:b], y[m][:].indirect(win_t[:, a // 16 : b // 16]), losers[m][:, a:b], SUBTRACT)
+            nc.vector.tensor_tensor(margin[m][:, a:b], y[m][:].indirect(entries(win_t, a, b)), losers[m][:, a:b], SUBTRACT)
 
-        def finish(m, a, b, queue=nc.sync):
+        def squash(m, a, b):
             nc.scalar.activation(result[m][:, a:b], margin[m][:, a:b], TANH, bias=bias[:])
-            queue.dma_start(out=out[m * P : (m + 1) * P, a:b], in_=result[m][:, a:b])
 
+        def store(m, a, b):
+            nc.sync.dma_start(out=out[m * P : (m + 1) * P, a:b], in_=result[m][:, a:b])
 
-        nc.vector.memset(planes[:].bitcast(I32), 0)
+        nc.vector.memset(scale_rows[:].bitcast(I32), 0)
         nc.vector.memset(zero[:], 0.0)
         nc.scalar.activation(bias[:], zero[:], TANH)
+
         load_words(0)
         nc.sync.dma_start(offs_t[:], offs)
-        load_w(0, 0)
-        load_scales()
-        load_w(0, 1)
+        load_piece(0, 0)
+        load_scale_rows()
+        load_piece(0, 1)
         load_words(1)
-        load_w(1, 0)
-        load_w(1, 1)
+        load_piece(1, 0)
+        load_piece(1, 1)
         nc.sync.dma_start(lose_t[:], lose)
         nc.sync.dma_start(win_t[:], win)
-        gather_words(0, 0, 512)
-        gather_planes(0, 512)
-        interleave(nc.scalar.copy, 0, 0)
-        interleave(nc.scalar.copy, 0, 1)
-        quantize(0, 2)
-        for a, b in pieces[0]:
+
+        gather_words(0, 0, S)
+        nc.vector.tensor_copy(picked_scales[:], scale_rows[:].indirect(offs_t[:]))
+        interleave_on_scalar(0, 0)
+        interleave_on_scalar(0, 1)
+        quantize(0, 2 * P, grouped_columns(0, 2 * P))
+        for a, b in RANGES[0]:
             multiply(0, 0, a, b)
-        interleave(nc.scalar.copy, 1, 0)
-        for a, b in pieces[0]:
+        interleave_on_scalar(1, 0)
+        for a, b in RANGES[0]:
             gather_words(1, a, b)
             multiply(0, 1, a, b)
             to_sbuf(0, a, b)
-        interleave(nc.vector.tensor_copy, 1, 1, 0, 64)
-        quantize(2)
-        late = keep.tile([P, 64 * PACK], BF16, name="late", tag="raw10", align_bytes=64)
-        nc.vector.tensor_copy(
-            late[:].rearrange("p (c i t) -> p c t i", i=4, t=PACK),
-            raw[1, 1][:, :, 64:128].rearrange("p t (c i) -> p c t i", i=4),
-        )
-        for a, b in pieces[1]:
+
+        third, last = first_column(1, 0), first_column(1, 1)
+        interleave(nc.vector.tensor_copy, grouped_columns(last, last + HALF), raw[1, 1][:, :, 0:HALF])
+        quantize(third, third + P, grouped_columns(third, third + P))
+        second_half = keep.tile([P, HALF * PACK], BF16, name="second_half", tag="raw10", align_bytes=64)
+        interleave(nc.vector.tensor_copy, second_half[:], raw[1, 1][:, :, HALF:P])
+        for a, b in RANGES[1]:
             multiply(1, 0, a, b)
-        nc.vector.quantize_mx(out=w_codes[:, 384:448].bitcast(FP8X4), scales=w_scales[:, 384:448], in_=grouped[:, 384 * PACK : 448 * PACK])
-        nc.vector.quantize_mx(out=w_codes[:, 448:512].bitcast(FP8X4), scales=w_scales[:, 448:512], in_=late[:])
-        for a, b in pieces[1]:
+        quantize(last, last + HALF, grouped_columns(last, last + HALF))
+        quantize(last + HALF, last + P, second_half[:])
+        for a, b in RANGES[1]:
             multiply(1, 1, a, b)
             to_sbuf(1, a, b)
+
         losers[0] = keep.tile([P, V], F32, name="losers0", tag="raw11", align_bytes=64)
-        fetch_losers(0, 0, 128)
-        fetch_losers(0, 128, 256)
-        subtract(0, 0, 128)
-        subtract(0, 128, 256)
-        finish(0, 0, 256)
-        fetch_losers(1, 0, 192)
-        fetch_losers(1, 192, 256)
-        subtract(1, 0, 192)
-        finish(1, 0, 192)
-        subtract(1, 192, 256)
-        finish(1, 192, 256)
+        middle = V // 2
+        fetch_losers(0, 0, middle)
+        fetch_losers(0, middle, V)
+        subtract(0, 0, middle)
+        subtract(0, middle, V)
+        squash(0, 0, V)
+        store(0, 0, V)
+        fetch_losers(1, 0, middle)
+        fetch_losers(1, middle, V)
+        subtract(1, 0, middle)
+        squash(1, 0, middle)
+        store(1, 0, middle)
+        for a in (middle, middle + V // 4):
+            subtract(1, a, a + V // 4)
+            squash(1, a, a + V // 4)
+        store(1, middle, V)

@@ -47,6 +47,7 @@ def tile_picked_ranknet_tanh_p_kernel(tc, x_words, x_scales, w1, offs, win, lose
         picked = [keep.tile([P, S], U32, name=f"picked{z}", align_bytes=64) for z in range(2)]
         picked_scales = keep.tile([P, S], U8, name="picked_scales", align_bytes=64)
         banks = {(m, a): psum.tile([P, b - a], F32, name=f"bank{m}_{a}") for m in range(2) for a, b in RANGES[m]}
+        spare_bank = psum.tile([P, S], F32, name="spare_bank")
         y = [keep.tile([P, S], F32, name=f"y{m}", align_bytes=64) for m in range(2)]
         losers = {1: keep.tile([P, V], F32, name="losers1", align_bytes=64)}
         margin = [keep.tile([P, V], F32, name=f"margin{m}", align_bytes=64) for m in range(2)]
@@ -136,12 +137,23 @@ def tile_picked_ranknet_tanh_p_kernel(tc, x_words, x_scales, w1, offs, win, lose
         nc.sync.dma_start(win_t[:], win)
 
         gather_words(0, 0, S)
-        nc.vector.tensor_copy(picked_scales[:], scale_rows[:].indirect(offs_t[:]))
         interleave_on_scalar(0, 0)
-        interleave_on_scalar(0, 1)
-        quantize(0, 2 * P, grouped_columns(0, 2 * P))
+        quantize(0, P, grouped_columns(0, P))
+        for a in (0, S // 2):
+            nc.vector.tensor_copy(picked_scales[:, a : a + S // 2], scale_rows[:].indirect(entries(offs_t, a, a + S // 2)))
         for a, b in RANGES[0]:
             multiply(0, 0, a, b)
+        nc.tensor.matmul_mx(
+            out=spare_bank[:],
+            lhsT=w_codes[:, 0:P].bitcast(FP8X4),
+            lhsT_scale=w_scales[:, 0:P],
+            rhs=picked[0][:].bitcast(FP8X4),
+            rhs_scale=picked_scales[:],
+            start=True,
+            stop=True,
+        )
+        interleave_on_scalar(0, 1)
+        quantize(P, 2 * P, grouped_columns(P, 2 * P))
         interleave_on_scalar(1, 0)
         for a, b in RANGES[0]:
             gather_words(1, a, b)

@@ -20,7 +20,6 @@ PACK = 4
 K_PASS = P * PACK
 PER_COLUMN = 16
 WALK = 4
-HALF = P // 2
 
 RANGES = {0: [(0, 256), (256, 384), (384, 512)], 1: [(a, a + P) for a in range(0, S, P)]}
 
@@ -161,15 +160,11 @@ def tile_picked_ranknet_tanh_p_kernel(tc, x_words, x_scales, w1, offs, win, lose
             to_sbuf(0, a, b)
 
         third, last = first_column(1, 0), first_column(1, 1)
-        interleave(nc.vector.tensor_copy, grouped_columns(last, last + HALF), raw[1, 1][:, :, 0:HALF])
+        interleave(nc.vector.tensor_copy, grouped_columns(last, last + P), raw[1, 1][:])
         quantize(third, third + P, grouped_columns(third, third + P))
-        second_half = keep.tile([P, HALF * PACK], BF16, name="second_half", tag="raw10", align_bytes=64)
-        interleave(nc.vector.tensor_copy, second_half[:], raw[1, 1][:, :, HALF:P])
+        quantize(last, last + P, grouped_columns(last, last + P))
         for a, b in RANGES[1]:
             multiply(1, 0, a, b)
-        quantize(last, last + HALF, grouped_columns(last, last + HALF))
-        quantize(last + HALF, last + P, second_half[:])
-        for a, b in RANGES[1]:
             multiply(1, 1, a, b)
             to_sbuf(1, a, b)
 

@@ -13,6 +13,7 @@ U16 = mybir.dt.uint16
 U8 = mybir.dt.uint8
 FP8X4 = mybir.dt.float8_e4m3fn_x4
 TANH = mybir.ActivationFunctionType.Tanh
+COPY = mybir.ActivationFunctionType.Copy
 SUBTRACT = mybir.AluOpType.subtract
 
 P = 128
@@ -21,7 +22,8 @@ K_PASS = P * PACK
 PER_COLUMN = 16
 WALK = 4
 
-RANGES = {0: [(0, 256), (256, 384), (384, 512)], 1: [(a, a + P) for a in range(0, S, P)]}
+RANGES = [(a, a + P) for a in range(0, S, P)]
+ON_VECTOR = ((0, 1), (0, 3), (1, 1))
 
 
 def tile_picked_ranknet_tanh_p_kernel(tc, x_words, x_scales, w1, offs, win, lose, out):
@@ -35,20 +37,17 @@ def tile_picked_ranknet_tanh_p_kernel(tc, x_words, x_scales, w1, offs, win, lose
         lose_t = keep.tile([P, V // PER_COLUMN], U16, name="lose_t")
         words = [keep.tile([P, T], I32, name=f"words{z}", align_bytes=64) for z in range(2)]
         scale_rows = keep.tile([P, T], U8, name="scale_rows", align_bytes=64)
-        raw = {
-            (m, z): keep.tile([P, PACK, P], F32, name=f"raw{m}{z}", tag=f"raw{m}{z}", align_bytes=64)
-            for m in range(2)
-            for z in range(2)
-        }
-        grouped = keep.tile([P, 4 * P * PACK], BF16, name="grouped", align_bytes=64)
-        w_codes = keep.tile([P, 4 * P], U32, name="w_codes", align_bytes=64)
+        raw_rows = keep.tile([P, PACK, N], F32, name="raw_rows", tag="raw_rows", align_bytes=64)
+        raw = {(m, 0): raw_rows[:, :, m * P : (m + 1) * P] for m in range(2)}
+        raw.update({(m, 1): keep.tile([P, PACK, P], F32, name=f"raw{m}", tag=f"raw{m}", align_bytes=64)[:] for m in range(2)})
+        grouped = {i: keep.tile([P, P * PACK], BF16, name=f"grouped{i}", align_bytes=64) for i in range(3)}
+        w_codes = {i: keep.tile([P, P], U32, name=f"w_codes{i}", align_bytes=64) for i in range(4)}
         w_scales = keep.tile([P, 4 * P], U8, name="w_scales", align_bytes=64)
         picked = [keep.tile([P, S], U32, name=f"picked{z}", align_bytes=64) for z in range(2)]
         picked_scales = keep.tile([P, S], U8, name="picked_scales", align_bytes=64)
-        banks = {(m, a): psum.tile([P, b - a], F32, name=f"bank{m}_{a}") for m in range(2) for a, b in RANGES[m]}
-        spare_bank = psum.tile([P, S], F32, name="spare_bank")
+        banks = {(m, a): psum.tile([P, b - a], F32, name=f"bank{m}_{a}") for m in range(2) for a, b in RANGES}
         y = [keep.tile([P, S], F32, name=f"y{m}", align_bytes=64) for m in range(2)]
-        losers = {1: keep.tile([P, V], F32, name="losers1", align_bytes=64)}
+        losers = [keep.tile([P, V], F32, name=f"losers{m}", align_bytes=64) for m in range(2)]
         margin = [keep.tile([P, V], F32, name=f"margin{m}", align_bytes=64) for m in range(2)]
         result = [keep.tile([P, V], F32, name=f"result{m}", align_bytes=64) for m in range(2)]
         zero = keep.tile([P, 1], F32, name="zero")
@@ -58,7 +57,7 @@ def tile_picked_ranknet_tanh_p_kernel(tc, x_words, x_scales, w1, offs, win, lose
             return list_tile[:, a // PER_COLUMN : b // PER_COLUMN]
 
         def first_column(m, z):
-            return (2 * m + z) * P
+            return (2 * z + m) * P
 
         def load_words(z):
             nc.sync.dma_start(out=words[z][:], in_=x_words[z].rearrange("p n t -> p (n t)").bitcast(I32))
@@ -70,12 +69,13 @@ def tile_picked_ranknet_tanh_p_kernel(tc, x_words, x_scales, w1, offs, win, lose
                     in_=x_scales[:, 4 * q : 4 * q + 4, :].bitcast(I32),
                 )
 
-        def load_piece(m, z):
-            rows = w1[z * K_PASS : (z + 1) * K_PASS, m * P : (m + 1) * P]
-            nc.sync.dma_start(out=raw[m, z][:], in_=rows.rearrange("(p t) c -> p t c", t=PACK))
+        def load_weights(target, z, a, b):
+            rows = w1[z * K_PASS : (z + 1) * K_PASS, a:b]
+            nc.sync.dma_start(out=target, in_=rows.rearrange("(p t) c -> p t c", t=PACK))
 
         def grouped_columns(a, b):
-            return grouped[:, a * PACK : b * PACK]
+            first = a // P * P
+            return grouped[a // P][:, (a - first) * PACK : (b - first) * PACK]
 
         def interleave(engine_copy, target, source):
             engine_copy(
@@ -83,12 +83,13 @@ def tile_picked_ranknet_tanh_p_kernel(tc, x_words, x_scales, w1, offs, win, lose
                 source.rearrange("p t (c i) -> p c t i", i=WALK),
             )
 
-        def interleave_on_scalar(m, z):
-            a = first_column(m, z)
-            interleave(nc.scalar.copy, grouped_columns(a, a + P), raw[m, z][:])
+        def interleave_piece(engine_copy, m, z, a=0, b=P):
+            first = first_column(m, z)
+            interleave(engine_copy, grouped_columns(first + a, first + b), raw[m, z][:, :, a:b])
 
-        def quantize(a, b, source):
-            nc.vector.quantize_mx(out=w_codes[:, a:b].bitcast(FP8X4), scales=w_scales[:, a:b], in_=source)
+        def quantize(m, z):
+            a = first_column(m, z)
+            nc.vector.quantize_mx(out=w_codes[a // P][:].bitcast(FP8X4), scales=w_scales[:, a : a + P], in_=grouped_columns(a, a + P))
 
         def gather_words(z, a, b):
             nc.vector.tensor_copy(picked[z][:, a:b], words[z][:].bitcast(U32).indirect(entries(offs_t, a, b)))
@@ -97,7 +98,7 @@ def tile_picked_ranknet_tanh_p_kernel(tc, x_words, x_scales, w1, offs, win, lose
             cols = slice(first_column(m, z), first_column(m, z) + P)
             nc.tensor.matmul_mx(
                 out=banks[m, a][:],
-                lhsT=w_codes[:, cols].bitcast(FP8X4),
+                lhsT=w_codes[2 * z + m][:].bitcast(FP8X4),
                 lhsT_scale=w_scales[:, cols],
                 rhs=picked[z][:, a:b].bitcast(FP8X4),
                 rhs_scale=picked_scales[4 * z : P, a:b],
@@ -105,10 +106,13 @@ def tile_picked_ranknet_tanh_p_kernel(tc, x_words, x_scales, w1, offs, win, lose
                 stop=(z == 1),
             )
 
-        def to_sbuf(m, a, b):
-            nc.scalar.copy(y[m][:, a:b], banks[m, a][:])
+        def to_sbuf(m, a, b, engine_copy=nc.scalar.copy):
+            engine_copy(y[m][:, a:b], banks[m, a][:])
 
         def fetch_losers(m, a, b):
+            nc.scalar.activation(losers[m][:, a:b], y[m][:].indirect(entries(lose_t, a, b)), COPY)
+
+        def fetch_losers_on_vector(m, a, b):
             nc.vector.tensor_copy(losers[m][:, a:b], y[m][:].indirect(entries(lose_t, a, b)))
 
         def subtract(m, a, b):
@@ -120,68 +124,57 @@ def tile_picked_ranknet_tanh_p_kernel(tc, x_words, x_scales, w1, offs, win, lose
         def store(m, a, b):
             nc.sync.dma_start(out=out[m * P : (m + 1) * P, a:b], in_=result[m][:, a:b])
 
-        nc.vector.memset(scale_rows[:].bitcast(I32), 0)
+        nc.vector.memset(scale_rows[:, 0 : T // 2].bitcast(I32), 0)
+        nc.gpsimd.memset(scale_rows[:, T // 2 : T].bitcast(I32), 0)
         nc.vector.memset(zero[:], 0.0)
         nc.scalar.activation(bias[:], zero[:], TANH)
 
         load_words(0)
         nc.sync.dma_start(offs_t[:], offs)
-        load_piece(0, 0)
         load_scale_rows()
-        load_piece(0, 1)
+        load_weights(raw_rows[:], 0, 0, N)
         load_words(1)
-        load_piece(1, 0)
-        load_piece(1, 1)
+        load_weights(raw[0, 1], 1, 0, P)
+        load_weights(raw[1, 1], 1, P, N)
         nc.sync.dma_start(lose_t[:], lose)
         nc.sync.dma_start(win_t[:], win)
 
         gather_words(0, 0, S)
-        interleave_on_scalar(0, 0)
-        quantize(0, P, grouped_columns(0, P))
-        for a in (0, S // 2):
-            nc.vector.tensor_copy(picked_scales[:, a : a + S // 2], scale_rows[:].indirect(entries(offs_t, a, a + S // 2)))
-        for a, b in RANGES[0]:
-            multiply(0, 0, a, b)
-        nc.tensor.matmul_mx(
-            out=spare_bank[:],
-            lhsT=w_codes[:, 0:P].bitcast(FP8X4),
-            lhsT_scale=w_scales[:, 0:P],
-            rhs=picked[0][:].bitcast(FP8X4),
-            rhs_scale=picked_scales[:],
-            start=True,
-            stop=True,
-        )
-        interleave_on_scalar(0, 1)
-        quantize(P, 2 * P, grouped_columns(P, 2 * P))
-        interleave_on_scalar(1, 0)
-        for a, b in RANGES[0]:
-            gather_words(1, a, b)
-            multiply(0, 1, a, b)
-            to_sbuf(0, a, b)
+        nc.vector.tensor_copy(picked_scales[:], scale_rows[:].indirect(offs_t[:]))
+        interleave_piece(nc.scalar.copy, 0, 0)
+        interleave_piece(nc.vector.tensor_copy, 1, 0, 0, P // 2)
+        interleave_piece(nc.scalar.copy, 1, 0, P // 2, P)
+        for m in range(2):
+            quantize(m, 0)
+            for a, b in RANGES:
+                multiply(m, 0, a, b)
+        gather_words(1, 0, S)
+        interleave_piece(nc.scalar.copy, 0, 1)
+        quantize(0, 1)
+        grouped[3] = keep.tile([P, P * PACK], BF16, name="grouped3", tag="raw0", align_bytes=64)
+        interleave_piece(nc.vector.tensor_copy, 1, 1, 0, P // 2)
+        interleave_piece(nc.scalar.copy, 1, 1, P // 2, P)
+        quantize(1, 1)
+        for m in range(2):
+            for i, (a, b) in enumerate(RANGES):
+                multiply(m, 1, a, b)
+                to_sbuf(m, a, b, nc.vector.tensor_copy if (m, i) in ON_VECTOR else nc.scalar.copy)
 
-        third, last = first_column(1, 0), first_column(1, 1)
-        interleave(nc.vector.tensor_copy, grouped_columns(last, last + P), raw[1, 1][:])
-        quantize(third, third + P, grouped_columns(third, third + P))
-        quantize(last, last + P, grouped_columns(last, last + P))
-        for a, b in RANGES[1]:
-            multiply(1, 0, a, b)
-            multiply(1, 1, a, b)
-            to_sbuf(1, a, b)
-
-        losers[0] = keep.tile([P, V], F32, name="losers0", tag="raw11", align_bytes=64)
-        middle = V // 2
-        fetch_losers(0, 0, middle)
+        middle, quarter = V // 2, V // 4
+        fetch_losers_on_vector(0, 0, quarter)
+        fetch_losers_on_vector(0, quarter, middle)
         fetch_losers(0, middle, V)
-        subtract(0, 0, middle)
+        fetch_losers(1, 0, middle)
+        fetch_losers(1, middle, V)
+        subtract(0, 0, quarter)
+        subtract(0, quarter, middle)
         subtract(0, middle, V)
         squash(0, 0, V)
         store(0, 0, V)
-        fetch_losers(1, 0, middle)
-        fetch_losers(1, middle, V)
         subtract(1, 0, middle)
         squash(1, 0, middle)
         store(1, 0, middle)
-        for a in (middle, middle + V // 4):
-            subtract(1, a, a + V // 4)
-            squash(1, a, a + V // 4)
+        for a in (middle, middle + quarter):
+            subtract(1, a, a + quarter)
+            squash(1, a, a + quarter)
         store(1, middle, V)

@@ -40,7 +40,7 @@ def tile_picked_ranknet_tanh_p_kernel(tc, x_words, x_scales, w1, offs, win, lose
         raw_rows = keep.tile([P, PACK, N], F32, name="raw_rows", tag="raw_rows", align_bytes=64)
         raw = {(m, 0): raw_rows[:, :, m * P : (m + 1) * P] for m in range(2)}
         raw.update({(m, 1): keep.tile([P, PACK, P], F32, name=f"raw{m}", tag=f"raw{m}", align_bytes=64)[:] for m in range(2)})
-        grouped = {i: keep.tile([P, P * PACK], BF16, name=f"grouped{i}", align_bytes=64) for i in range(3)}
+        grouped = {i: keep.tile([P, P * PACK], BF16, name=f"grouped{i}", align_bytes=64) for i in range(4)}
         w_codes = {i: keep.tile([P, P], U32, name=f"w_codes{i}", align_bytes=64) for i in range(4)}
         w_scales = keep.tile([P, 4 * P], U8, name="w_scales", align_bytes=64)
         picked = [keep.tile([P, S], U32, name=f"picked{z}", align_bytes=64) for z in range(2)]
@@ -150,10 +150,9 @@ def tile_picked_ranknet_tanh_p_kernel(tc, x_words, x_scales, w1, offs, win, lose
                 multiply(m, 0, a, b)
         gather_words(1, 0, S)
         interleave_piece(nc.scalar.copy, 0, 1)
-        quantize(0, 1)
-        grouped[3] = keep.tile([P, P * PACK], BF16, name="grouped3", tag="raw0", align_bytes=64)
         interleave_piece(nc.vector.tensor_copy, 1, 1, 0, P // 2)
         interleave_piece(nc.scalar.copy, 1, 1, P // 2, P)
+        quantize(0, 1)
         quantize(1, 1)
         for m in range(2):
             for i, (a, b) in enumerate(RANGES):

@@ -106,6 +106,17 @@ def tile_picked_ranknet_tanh_p_kernel(tc, x_words, x_scales, w1, offs, win, lose
                 stop=(z == 1),
             )
 
+        def warm_up(columns):
+            nc.tensor.matmul_mx(
+                out=banks[1, S - P][:, 0:columns],
+                lhsT=w_codes[0][:].bitcast(FP8X4),
+                lhsT_scale=w_scales[:, 0:P],
+                rhs=w_codes[0][:, 0:columns].bitcast(FP8X4),
+                rhs_scale=w_scales[:, 0:columns],
+                start=True,
+                stop=True,
+            )
+
         def to_sbuf(m, a, b, engine_copy=nc.scalar.copy):
             engine_copy(y[m][:, a:b], banks[m, a][:])
 
@@ -144,10 +155,14 @@ def tile_picked_ranknet_tanh_p_kernel(tc, x_words, x_scales, w1, offs, win, lose
         interleave_piece(nc.scalar.copy, 0, 0)
         interleave_piece(nc.vector.tensor_copy, 1, 0, 0, P // 2)
         interleave_piece(nc.scalar.copy, 1, 0, P // 2, P)
-        for m in range(2):
-            quantize(m, 0)
-            for a, b in RANGES:
-                multiply(m, 0, a, b)
+        quantize(0, 0)
+        warm_up(P)
+        warm_up(P // 2)
+        for a, b in RANGES:
+            multiply(0, 0, a, b)
+        quantize(1, 0)
+        for a, b in RANGES:
+            multiply(1, 0, a, b)
         gather_words(1, 0, S)
         interleave_piece(nc.scalar.copy, 0, 1)
         interleave_piece(nc.vector.tensor_copy, 1, 1, 0, P // 2)

@@ -183,8 +183,9 @@ def tile_picked_ranknet_tanh_p_kernel(tc, x_words, x_scales, w1, offs, win, lose
         subtract(0, 0, quarter)
         subtract(0, quarter, middle)
         subtract(0, middle, V)
-        squash(0, 0, V)
-        store(0, 0, V)
+        for a in (0, middle):
+            squash(0, a, a + middle)
+            store(0, a, a + middle)
         subtract(1, 0, middle)
         squash(1, 0, middle)
         store(1, 0, middle)

@@ -106,17 +106,6 @@ def tile_picked_ranknet_tanh_p_kernel(tc, x_words, x_scales, w1, offs, win, lose
                 stop=(z == 1),
             )
 
-        def warm_up(columns):
-            nc.tensor.matmul_mx(
-                out=banks[1, S - P][:, 0:columns],
-                lhsT=w_codes[0][:].bitcast(FP8X4),
-                lhsT_scale=w_scales[:, 0:P],
-                rhs=w_codes[0][:, 0:columns].bitcast(FP8X4),
-                rhs_scale=w_scales[:, 0:columns],
-                start=True,
-                stop=True,
-            )
-
         def to_sbuf(m, a, b, engine_copy=nc.scalar.copy):
             engine_copy(y[m][:, a:b], banks[m, a][:])
 
@@ -155,14 +144,10 @@ def tile_picked_ranknet_tanh_p_kernel(tc, x_words, x_scales, w1, offs, win, lose
         interleave_piece(nc.scalar.copy, 0, 0)
         interleave_piece(nc.vector.tensor_copy, 1, 0, 0, P // 2)
         interleave_piece(nc.scalar.copy, 1, 0, P // 2, P)
-        quantize(0, 0)
-        warm_up(P)
-        warm_up(P // 2)
-        for a, b in RANGES:
-            multiply(0, 0, a, b)
-        quantize(1, 0)
-        for a, b in RANGES:
-            multiply(1, 0, a, b)
+        for m in range(2):
+            quantize(m, 0)
+            for a, b in RANGES:
+                multiply(m, 0, a, b)
         gather_words(1, 0, S)
         interleave_piece(nc.scalar.copy, 0, 1)
         interleave_piece(nc.vector.tensor_copy, 1, 1, 0, P // 2)

@@ -23,7 +23,7 @@ PER_COLUMN = 16
 WALK = 4
 
 RANGES = [(a, a + P) for a in range(0, S, P)]
-ON_VECTOR = ((0, 1), (0, 3), (1, 1))
+ON_VECTOR = ((0, 0), (0, 1), (1, 0))
 
 
 def tile_picked_ranknet_tanh_p_kernel(tc, x_words, x_scales, w1, offs, win, lose, out):

@@ -23,7 +23,6 @@ PER_COLUMN = 16
 WALK = 4
 
 RANGES = [(a, a + P) for a in range(0, S, P)]
-ON_VECTOR = ((0, 0), (0, 1), (1, 0))
 
 
 def tile_picked_ranknet_tanh_p_kernel(tc, x_words, x_scales, w1, offs, win, lose, out):
@@ -37,12 +36,13 @@ def tile_picked_ranknet_tanh_p_kernel(tc, x_words, x_scales, w1, offs, win, lose
         lose_t = keep.tile([P, V // PER_COLUMN], U16, name="lose_t")
         words = [keep.tile([P, T], I32, name=f"words{z}", align_bytes=64) for z in range(2)]
         scale_rows = keep.tile([P, T], U8, name="scale_rows", align_bytes=64)
-        raw_rows = keep.tile([P, PACK, N], F32, name="raw_rows", tag="raw_rows", align_bytes=64)
+        raw_rows = keep.tile([P, PACK, N], F32, name="raw_rows", align_bytes=64)
         raw = {(m, 0): raw_rows[:, :, m * P : (m + 1) * P] for m in range(2)}
-        raw.update({(m, 1): keep.tile([P, PACK, P], F32, name=f"raw{m}", tag=f"raw{m}", align_bytes=64)[:] for m in range(2)})
-        grouped = {i: keep.tile([P, P * PACK], BF16, name=f"grouped{i}", align_bytes=64) for i in range(4)}
-        w_codes = {i: keep.tile([P, P], U32, name=f"w_codes{i}", align_bytes=64) for i in range(4)}
-        w_scales = keep.tile([P, 4 * P], U8, name="w_scales", align_bytes=64)
+        raw.update({(m, 1): keep.tile([P, PACK, P], F32, name=f"raw{m}", align_bytes=64)[:] for m in range(2)})
+        pieces = [(m, z) for z in range(2) for m in range(2)]
+        grouped = {mz: keep.tile([P, P * PACK], BF16, name=f"grouped{mz[0]}{mz[1]}", align_bytes=64) for mz in pieces}
+        w_codes = {mz: keep.tile([P, P], U32, name=f"w_codes{mz[0]}{mz[1]}", align_bytes=64) for mz in pieces}
+        w_scales = {mz: keep.tile([P, P], U8, name=f"w_scales{mz[0]}{mz[1]}", align_bytes=64) for mz in pieces}
         picked = [keep.tile([P, S], U32, name=f"picked{z}", align_bytes=64) for z in range(2)]
         picked_scales = keep.tile([P, S], U8, name="picked_scales", align_bytes=64)
         banks = {(m, a): psum.tile([P, b - a], F32, name=f"bank{m}_{a}") for m in range(2) for a, b in RANGES}
@@ -55,9 +55,6 @@ def tile_picked_ranknet_tanh_p_kernel(tc, x_words, x_scales, w1, offs, win, lose
 
         def entries(list_tile, a, b):
             return list_tile[:, a // PER_COLUMN : b // PER_COLUMN]
-
-        def first_column(m, z):
-            return (2 * z + m) * P
 
         def load_words(z):
             nc.sync.dma_start(out=words[z][:], in_=x_words[z].rearrange("p n t -> p (n t)").bitcast(I32))
@@ -73,46 +70,39 @@ def tile_picked_ranknet_tanh_p_kernel(tc, x_words, x_scales, w1, offs, win, lose
             rows = w1[z * K_PASS : (z + 1) * K_PASS, a:b]
             nc.sync.dma_start(out=target, in_=rows.rearrange("(p t) c -> p t c", t=PACK))
 
-        def grouped_columns(a, b):
-            first = a // P * P
-            return grouped[a // P][:, (a - first) * PACK : (b - first) * PACK]
-
-        def interleave(engine_copy, target, source):
+        def interleave(engine_copy, m, z, a=0, b=P):
             engine_copy(
-                target.rearrange("p (c i t) -> p c t i", i=WALK, t=PACK),
-                source.rearrange("p t (c i) -> p c t i", i=WALK),
+                grouped[m, z][:, a * PACK : b * PACK].rearrange("p (c i t) -> p c t i", i=WALK, t=PACK),
+                raw[m, z][:, :, a:b].rearrange("p t (c i) -> p c t i", i=WALK),
             )
 
-        def interleave_piece(engine_copy, m, z, a=0, b=P):
-            first = first_column(m, z)
-            interleave(engine_copy, grouped_columns(first + a, first + b), raw[m, z][:, :, a:b])
-
         def quantize(m, z):
-            a = first_column(m, z)
-            nc.vector.quantize_mx(out=w_codes[a // P][:].bitcast(FP8X4), scales=w_scales[:, a : a + P], in_=grouped_columns(a, a + P))
+            nc.vector.quantize_mx(out=w_codes[m, z][:].bitcast(FP8X4), scales=w_scales[m, z][:], in_=grouped[m, z][:])
 
         def gather_words(z, a, b):
             nc.vector.tensor_copy(picked[z][:, a:b], words[z][:].bitcast(U32).indirect(entries(offs_t, a, b)))
 
+        def gather_bytes(a, b):
+            nc.vector.tensor_copy(picked_scales[:, a:b], scale_rows[:].indirect(entries(offs_t, a, b)))
+
         def multiply(m, z, a, b):
-            cols = slice(first_column(m, z), first_column(m, z) + P)
             nc.tensor.matmul_mx(
                 out=banks[m, a][:],
-                lhsT=w_codes[2 * z + m][:].bitcast(FP8X4),
-                lhsT_scale=w_scales[:, cols],
+                lhsT=w_codes[m, z][:].bitcast(FP8X4),
+                lhsT_scale=w_scales[m, z][:],
                 rhs=picked[z][:, a:b].bitcast(FP8X4),
                 rhs_scale=picked_scales[4 * z : P, a:b],
                 start=(z == 0),
                 stop=(z == 1),
             )
 
-        def to_sbuf(m, a, b, engine_copy=nc.scalar.copy):
+        def to_sbuf(engine_copy, m, a, b):
             engine_copy(y[m][:, a:b], banks[m, a][:])
 
-        def fetch_losers(m, a, b):
+        def losers_on_scalar(m, a, b):
             nc.scalar.activation(losers[m][:, a:b], y[m][:].indirect(entries(lose_t, a, b)), COPY)
 
-        def fetch_losers_on_vector(m, a, b):
+        def losers_on_vector(m, a, b):
             nc.vector.tensor_copy(losers[m][:, a:b], y[m][:].indirect(entries(lose_t, a, b)))
 
         def subtract(m, a, b):
@@ -128,6 +118,8 @@ def tile_picked_ranknet_tanh_p_kernel(tc, x_words, x_scales, w1, offs, win, lose
         nc.gpsimd.memset(scale_rows[:, T // 2 : T].bitcast(I32), 0)
         nc.vector.memset(zero[:], 0.0)
         nc.scalar.activation(bias[:], zero[:], TANH)
+        on_scalar, on_vector = nc.scalar.copy, nc.vector.tensor_copy
+        middle, quarter = V // 2, V // 4
 
         load_words(0)
         nc.sync.dma_start(offs_t[:], offs)
@@ -140,31 +132,33 @@ def tile_picked_ranknet_tanh_p_kernel(tc, x_words, x_scales, w1, offs, win, lose
         nc.sync.dma_start(win_t[:], win)
 
         gather_words(0, 0, S)
-        nc.vector.tensor_copy(picked_scales[:], scale_rows[:].indirect(offs_t[:]))
-        interleave_piece(nc.scalar.copy, 0, 0)
-        interleave_piece(nc.vector.tensor_copy, 1, 0, 0, P // 2)
-        interleave_piece(nc.scalar.copy, 1, 0, P // 2, P)
+        gather_bytes(0, S)
+        interleave(on_scalar, 0, 0)
+        interleave(on_vector, 1, 0, 0, P // 2)
+        interleave(on_scalar, 1, 0, P // 2, P)
         for m in range(2):
             quantize(m, 0)
             for a, b in RANGES:
                 multiply(m, 0, a, b)
         gather_words(1, 0, S)
-        interleave_piece(nc.scalar.copy, 0, 1)
-        interleave_piece(nc.vector.tensor_copy, 1, 1, 0, P // 2)
-        interleave_piece(nc.scalar.copy, 1, 1, P // 2, P)
+        interleave(on_scalar, 0, 1)
+        interleave(on_vector, 1, 1, 0, P // 2)
+        interleave(on_scalar, 1, 1, P // 2, P)
         quantize(0, 1)
         quantize(1, 1)
         for m in range(2):
             for i, (a, b) in enumerate(RANGES):
                 multiply(m, 1, a, b)
-                to_sbuf(m, a, b, nc.vector.tensor_copy if (m, i) in ON_VECTOR else nc.scalar.copy)
+                to_sbuf(on_vector if (m, i) in ((0, 0), (0, 2), (1, 0), (1, 1)) else on_scalar, m, a, b)
 
-        middle, quarter = V // 2, V // 4
-        fetch_losers_on_vector(0, 0, quarter)
-        fetch_losers_on_vector(0, quarter, middle)
-        fetch_losers(0, middle, V)
-        fetch_losers(1, 0, middle)
-        fetch_losers(1, middle, V)
+        losers_on_vector(0, 0, quarter)
+        losers_on_vector(0, quarter, middle)
+        losers_on_scalar(0, middle, V)
+        losers_on_scalar(1, 0, middle)
+        losers_on_scalar(1, middle, V)
+        last = V - quarter
+        winners = keep.tile([P, quarter], F32, name="winners", align_bytes=64)
+        nc.scalar.activation(winners[:], y[1][:].indirect(entries(win_t, last, V)), COPY)
         subtract(0, 0, quarter)
         subtract(0, quarter, middle)
         subtract(0, middle, V)
@@ -174,7 +168,8 @@ def tile_picked_ranknet_tanh_p_kernel(tc, x_words, x_scales, w1, offs, win, lose
         subtract(1, 0, middle)
         squash(1, 0, middle)
         store(1, 0, middle)
-        for a in (middle, middle + quarter):
-            subtract(1, a, a + quarter)
-            squash(1, a, a + quarter)
+        subtract(1, middle, last)
+        squash(1, middle, last)
+        nc.vector.tensor_tensor(margin[1][:, last:V], winners[:], losers[1][:, last:V], SUBTRACT)
+        squash(1, last, V)
         store(1, middle, V)

@@ -156,9 +156,6 @@ def tile_picked_ranknet_tanh_p_kernel(tc, x_words, x_scales, w1, offs, win, lose
         losers_on_scalar(0, middle, V)
         losers_on_scalar(1, 0, middle)
         losers_on_scalar(1, middle, V)
-        last = V - quarter
-        winners = keep.tile([P, quarter], F32, name="winners", align_bytes=64)
-        nc.scalar.activation(winners[:], y[1][:].indirect(entries(win_t, last, V)), COPY)
         subtract(0, 0, quarter)
         subtract(0, quarter, middle)
         subtract(0, middle, V)
@@ -168,8 +165,7 @@ def tile_picked_ranknet_tanh_p_kernel(tc, x_words, x_scales, w1, offs, win, lose
         subtract(1, 0, middle)
         squash(1, 0, middle)
         store(1, 0, middle)
-        subtract(1, middle, last)
-        squash(1, middle, last)
-        nc.vector.tensor_tensor(margin[1][:, last:V], winners[:], losers[1][:, last:V], SUBTRACT)
-        squash(1, last, V)
+        for a in (middle, middle + quarter):
+            subtract(1, a, a + quarter)
+            squash(1, a, a + quarter)
         store(1, middle, V)

from contextlib import ExitStack

import concourse.mybir as mybir

K, T, S, V, N = 1024, 1024, 512, 256, 256
FLOPS = 2 * K * S * N

F32 = mybir.dt.float32
BF16 = mybir.dt.bfloat16
I32 = mybir.dt.int32
U32 = mybir.dt.uint32
U16 = mybir.dt.uint16
U8 = mybir.dt.uint8
FP8X4 = mybir.dt.float8_e4m3fn_x4
TANH = mybir.ActivationFunctionType.Tanh
COPY = mybir.ActivationFunctionType.Copy
SUBTRACT = mybir.AluOpType.subtract

P = 128
PACK = 4
K_PASS = P * PACK
PER_COLUMN = 16
WALK = 4

RANGES = [(a, a + P) for a in range(0, S, P)]


def tile_picked_ranknet_tanh_p_kernel(tc, x_words, x_scales, w1, offs, win, lose, out):
    nc = tc.nc
    with ExitStack() as ctx:
        keep = ctx.enter_context(tc.tile_pool(name="keep", bufs=1))
        psum = ctx.enter_context(tc.psum_pool(name="psum", bufs=1))

        offs_t = keep.tile([P, S // PER_COLUMN], U16, name="offs_t")
        win_t = keep.tile([P, V // PER_COLUMN], U16, name="win_t")
        lose_t = keep.tile([P, V // PER_COLUMN], U16, name="lose_t")
        words = [keep.tile([P, T], I32, name=f"words{z}", align_bytes=64) for z in range(2)]
        scale_rows = keep.tile([P, T], U8, name="scale_rows", align_bytes=64)
        raw_rows = keep.tile([P, PACK, N], F32, name="raw_rows", align_bytes=64)
        raw = {(m, 0): raw_rows[:, :, m * P : (m + 1) * P] for m in range(2)}
        raw.update({(m, 1): keep.tile([P, PACK, P], F32, name=f"raw{m}", align_bytes=64)[:] for m in range(2)})
        pieces = [(m, z) for z in range(2) for m in range(2)]
        grouped = {mz: keep.tile([P, P * PACK], BF16, name=f"grouped{mz[0]}{mz[1]}", align_bytes=64) for mz in pieces}
        w_codes = {mz: keep.tile([P, P], U32, name=f"w_codes{mz[0]}{mz[1]}", align_bytes=64) for mz in pieces}
        w_scales = {mz: keep.tile([P, P], U8, name=f"w_scales{mz[0]}{mz[1]}", align_bytes=64) for mz in pieces}
        picked = [keep.tile([P, S], U32, name=f"picked{z}", align_bytes=64) for z in range(2)]
        picked_scales = keep.tile([P, S], U8, name="picked_scales", align_bytes=64)
        banks = {(m, a): psum.tile([P, b - a], F32, name=f"bank{m}_{a}") for m in range(2) for a, b in RANGES}
        y = [keep.tile([P, S], F32, name=f"y{m}", align_bytes=64) for m in range(2)]
        losers = [keep.tile([P, V], F32, name=f"losers{m}", align_bytes=64) for m in range(2)]
        margin = [keep.tile([P, V], F32, name=f"margin{m}", align_bytes=64) for m in range(2)]
        result = [keep.tile([P, V], F32, name=f"result{m}", align_bytes=64) for m in range(2)]
        zero = keep.tile([P, 1], F32, name="zero")
        bias = keep.tile([P, 1], F32, name="bias")

        def entries(list_tile, a, b):
            return list_tile[:, a // PER_COLUMN : b // PER_COLUMN]

        def load_words(z):
            nc.sync.dma_start(out=words[z][:], in_=x_words[z].rearrange("p n t -> p (n t)").bitcast(I32))

        def load_scale_rows():
            for q in range(4):
                nc.sync.dma_start(
                    out=scale_rows[32 * q : 32 * q + 8, :].bitcast(I32),
                    in_=x_scales[:, 4 * q : 4 * q + 4, :].bitcast(I32),
                )

        def load_weights(target, z, a, b):
            rows = w1[z * K_PASS : (z + 1) * K_PASS, a:b]
            nc.sync.dma_start(out=target, in_=rows.rearrange("(p t) c -> p t c", t=PACK))

        def interleave(engine_copy, m, z, a=0, b=P):
            engine_copy(
                grouped[m, z][:, a * PACK : b * PACK].rearrange("p (c i t) -> p c t i", i=WALK, t=PACK),
                raw[m, z][:, :, a:b].rearrange("p t (c i) -> p c t i", i=WALK),
            )

        def quantize(m, z):
            nc.vector.quantize_mx(out=w_codes[m, z][:].bitcast(FP8X4), scales=w_scales[m, z][:], in_=grouped[m, z][:])

        def gather_words(z, a, b):
            nc.vector.tensor_copy(picked[z][:, a:b], words[z][:].bitcast(U32).indirect(entries(offs_t, a, b)))

        def gather_bytes(a, b):
            nc.vector.tensor_copy(picked_scales[:, a:b], scale_rows[:].indirect(entries(offs_t, a, b)))

        def multiply(m, z, a, b):
            nc.tensor.matmul_mx(
                out=banks[m, a][:],
                lhsT=w_codes[m, z][:].bitcast(FP8X4),
                lhsT_scale=w_scales[m, z][:],
                rhs=picked[z][:, a:b].bitcast(FP8X4),
                rhs_scale=picked_scales[4 * z : P, a:b],
                start=(z == 0),
                stop=(z == 1),
            )

        def to_sbuf(engine_copy, m, a, b):
            engine_copy(y[m][:, a:b], banks[m, a][:])

        def losers_on_scalar(m, a, b):
            nc.scalar.activation(losers[m][:, a:b], y[m][:].indirect(entries(lose_t, a, b)), COPY)

        def losers_on_vector(m, a, b):
            nc.vector.tensor_copy(losers[m][:, a:b], y[m][:].indirect(entries(lose_t, a, b)))

        def subtract(m, a, b):
            nc.vector.tensor_tensor(margin[m][:, a:b], y[m][:].indirect(entries(win_t, a, b)), losers[m][:, a:b], SUBTRACT)

        def squash(m, a, b):
            nc.scalar.activation(result[m][:, a:b], margin[m][:, a:b], TANH, bias=bias[:])

        def store(m, a, b):
            nc.sync.dma_start(out=out[m * P : (m + 1) * P, a:b], in_=result[m][:, a:b])

        nc.vector.memset(scale_rows[:, 0 : T // 2].bitcast(I32), 0)
        nc.gpsimd.memset(scale_rows[:, T // 2 : T].bitcast(I32), 0)
        nc.vector.memset(zero[:], 0.0)
        nc.scalar.activation(bias[:], zero[:], TANH)
        on_scalar, on_vector = nc.scalar.copy, nc.vector.tensor_copy
        middle, quarter = V // 2, V // 4

        load_words(0)
        nc.sync.dma_start(offs_t[:], offs)
        load_scale_rows()
        load_weights(raw_rows[:], 0, 0, N)
        load_words(1)
        load_weights(raw[0, 1], 1, 0, P)
        load_weights(raw[1, 1], 1, P, N)
        nc.sync.dma_start(lose_t[:], lose)
        nc.sync.dma_start(win_t[:], win)

        gather_words(0, 0, S)
        gather_bytes(0, S)
        interleave(on_scalar, 0, 0)
        interleave(on_vector, 1, 0, 0, P // 2)
        interleave(on_scalar, 1, 0, P // 2, P)
        for m in range(2):
            quantize(m, 0)
            for a, b in RANGES:
                multiply(m, 0, a, b)
        gather_words(1, 0, S)
        interleave(on_scalar, 0, 1)
        interleave(on_vector, 1, 1, 0, P // 2)
        interleave(on_scalar, 1, 1, P // 2, P)
        quantize(0, 1)
        quantize(1, 1)
        for m in range(2):
            for i, (a, b) in enumerate(RANGES):
                multiply(m, 1, a, b)
                to_sbuf(on_vector if (m, i) in ((0, 0), (0, 2), (1, 0), (1, 1)) else on_scalar, m, a, b)

        losers_on_vector(0, 0, quarter)
        losers_on_vector(0, quarter, middle)
        losers_on_scalar(0, middle, V)
        losers_on_scalar(1, 0, middle)
        losers_on_scalar(1, middle, V)
        subtract(0, 0, quarter)
        subtract(0, quarter, middle)
        subtract(0, middle, V)
        for a in (0, middle):
            squash(0, a, a + middle)
            store(0, a, a + middle)
        subtract(1, 0, middle)
        squash(1, 0, middle)
        store(1, 0, middle)
        for a in (middle, middle + quarter):
            subtract(1, a, a + quarter)
            squash(1, a, a + quarter)
        store(1, middle, V)
